import numpy as np
import ml_dtypes


def mxq(x, axis, fmt="e4m3"):
    dtype, down = {"e4m3": (ml_dtypes.float8_e4m3fn, 7), "e5m2": (ml_dtypes.float8_e5m2, 14)}[fmt]
    v = np.moveaxis(np.asarray(x, np.float32).astype(ml_dtypes.bfloat16).astype(np.float64), axis, -1)
    blocks = v.reshape(v.shape[:-1] + (-1, 32))
    amax = np.abs(blocks).max(-1, keepdims=True)
    byte = np.maximum(np.where(amax > 0, np.frexp(amax)[1] - 1 + 127, 0) - down, 1)
    scale = np.exp2(byte - 127.0)
    codes = (blocks / scale).astype(np.float32).astype(dtype).astype(np.float64)
    return np.moveaxis((codes * scale).reshape(v.shape), -1, axis)


WIDE = False


def mx_kscale(k):
    if not WIDE:
        return np.ones(k)
    levels = np.array([10, -10, 5, -5, 0])
    if k % 512:
        return np.exp2(np.random.permutation(np.resize(levels, k // 32))).repeat(32)
    a = np.empty((k // 512, 16))
    for p in range(k // 512):
        a[p, :8] = np.random.permutation(np.resize(levels, 8))
        for g in range(8):
            far = levels[np.abs(levels - a[p, g]) >= 10]
            a[p, g + 8] = far[np.random.randint(len(far))]
    return np.exp2(a.ravel()).repeat(32)


BF16 = ml_dtypes.bfloat16


def bf(x):
    return np.asarray(x, np.float32).astype(BF16)


def f64(x):
    return np.asarray(x).astype(np.float64)


E2M1 = np.array([0.0, 0.5, 1.0, 1.5, 2.0, 3.0, 4.0, 6.0, -0.0, -0.5, -1.0, -1.5, -2.0, -3.0, -4.0, -6.0])


def pack_weight(w, fmt):
    k, n = w.shape
    w = f64(bf(w)).reshape(k // 32, 32, n)
    amax = np.abs(w).max(1)
    if fmt == "e4m3":
        byte = np.frexp(amax)[1] - 1 + 127 - 7
    else:
        mant, ex = np.frexp(amax / 6.0)
        byte = np.where(mant > 0.5, ex, ex - 1) + 127
    byte = np.clip(np.where(amax > 0, byte, 1), 1, 254)
    scaled = (w * np.exp2(127.0 - byte)[:, None, :]).reshape(k, n).astype(np.float32)
    by_word = np.ascontiguousarray(scaled.reshape(k // 512, 128, 4, n).transpose(0, 1, 3, 2))
    if fmt == "e4m3":
        words = by_word.astype(ml_dtypes.float8_e4m3fn).view(np.uint8)
    else:
        c = by_word.astype(ml_dtypes.float4_e2m1fn).view(np.uint8) & 0xF
        words = c[..., 0::2] | (c[..., 1::2] << 4)
    return np.ascontiguousarray(words), np.ascontiguousarray(byte.astype(np.uint8).reshape(k // 512, 16, n))


def unpack_weight(words, scales, fmt):
    g, p, n, _ = words.shape
    if fmt == "e4m3":
        vals = np.ascontiguousarray(words).view(ml_dtypes.float8_e4m3fn).astype(np.float64)
    else:
        nib = np.empty((g, p, n, 4), np.uint8)
        nib[..., 0::2] = words & 0xF
        nib[..., 1::2] = words >> 4
        vals = E2M1[nib]
    vals = vals * np.repeat(np.exp2(scales.astype(np.float64) - 127.0), 8, axis=1)[..., None]
    return vals.transpose(0, 1, 3, 2).reshape(g * 512, n)
def pack4(w):
    words, scales = pack_weight(w, "e2m1")
    return words.reshape(words.shape[0], 128, -1), scales


def unpack4(words, scales):
    return unpack_weight(words.reshape(words.shape[0], 128, -1, 2), scales, "e2m1")


E4M3FN = np.array([(-1.0 if i & 128 else 1.0) * ((1.0 + (i & 7) / 8.0) * 2.0 ** (((i >> 3) & 15) - 7) if i & 120 else (i & 7) * 2.0 ** -9) for i in range(256)])


def e4m3fn_bytes(y):
    return np.clip(np.asarray(y, np.float64), -448.0, 448.0).astype(np.float32).astype(ml_dtypes.float8_e4m3fn).view(np.uint8)


def e4m3fn_values(b):
    return E4M3FN[b]


B, S, T, D, V = 2, 256, 512, 512, 1024


def draw0():
    a, t = mx_kscale(D), mx_kscale(D)
    h = bf(np.random.standard_normal((B, T, D)) * a)
    wc_words, wc_scales = pack4(np.random.standard_normal((D, D)) / np.sqrt(D) / a[:, None])
    g = bf((1.0 + 0.25 * np.random.standard_normal(D)) * t)
    s = bf(np.random.standard_normal((B, S, D)) / t)
    wo_words, wo_scales = pack4(np.random.standard_normal((D, V)) / np.sqrt(D) * t[:, None])
    bo = bf(0.5 * np.random.standard_normal(V))
    return {"h": h, "wc_words": wc_words, "wc_scales": wc_scales, "g": g, "s": s, "wo_words": wo_words, "wo_scales": wo_scales, "bo": bo}


def copy_keys(h, wc_words, wc_scales, g):
    p = mxq(f64(h), 2, "e4m3") @ unpack4(wc_words, wc_scales)
    return np.tanh(p) * f64(g)


def log_lift(z):
    n = z.shape[-1]
    m = z.max(-1, keepdims=True)
    lse = m + np.log(np.sum(np.exp(z - m), axis=-1, keepdims=True))
    return z - lse + np.log(n)


def core(h, wc_words, wc_scales, g, s, wo_words, wo_scales, bo):
    k = copy_keys(h, wc_words, wc_scales, g)
    sq = mxq(f64(s), 2, "e4m3")
    cp = (sq @ mxq(k, 2, "e4m3").transpose(0, 2, 1)) / np.sqrt(D)
    gen = (sq @ unpack4(wo_words, wo_scales)) + f64(bo)
    z = np.concatenate([gen, cp], axis=-1)
    return log_lift(z)


def setup_inputs():
    drawn = draw0()
    full = np.asarray(drawn['h']).astype(np.float64)
    scale = (np.abs(full).reshape(2, 4, 128, 4, 128).max(axis=(2, 4)) / 448.0).astype(np.float32)
    given = {}
    for key, value in drawn.items():
        if key == 'h':
            given['h_bytes'] = e4m3fn_bytes(full / np.repeat(np.repeat(scale.astype(np.float64), 128, axis=1), 128, axis=2))
            given['h_scale'] = scale
        else:
            given[key] = value
    return given


def reference(h_bytes, h_scale, wc_words, wc_scales, g, s, wo_words, wo_scales, bo):
    return core(e4m3fn_values(h_bytes) * np.repeat(np.repeat(h_scale.astype(np.float64), 128, axis=1), 128, axis=2), wc_words, wc_scales, g, s, wo_words, wo_scales, bo)

@@ -1,0 +1,522 @@
+import math
+from contextlib import ExitStack
+
+import concourse.mybir as mybir
+from concourse.masks import make_identity
+
+B, S, T, D, V = 2, 256, 512, 512, 1024
+FLOPS = 2 * B * (T * D * D + S * T * D + S * D * V)
+
+F32 = mybir.dt.float32
+BF16 = mybir.dt.bfloat16
+I32 = mybir.dt.int32
+U32 = mybir.dt.uint32
+U8 = mybir.dt.uint8
+FP8 = mybir.dt.float8_e4m3fn
+FP8X4 = mybir.dt.float8_e4m3fn_x4
+FP4X4 = mybir.dt.float4_e2m1fn_x4
+ALU = mybir.AluOpType
+ACT = mybir.ActivationFunctionType
+AX = mybir.AxisListType
+
+P = 128
+PACK = 4
+BANK = 512
+Z = V + T
+TERMS = 30
+CENTRE = 3.25
+EXP_MASK = 0x7F800000
+NCOL = TERMS + 3
+
+ORDER = (
+    ("load_s", 0),
+    ("load_h", 0, 0),
+    ("zero", "bo"),
+    ("load_bo", "y"),
+    ("zero", "wcs"),
+    ("constants",),
+    ("load_hs", "y"),
+    ("load_h", 0, 1),
+    ("zero", "wos"),
+    ("load_g", "y"),
+    ("load_wos", 3, "g"),
+    ("constant_term",),
+    ("identity",),
+    ("coefficients",),
+    ("load_wos", 0, "y"),
+    ("load_wos", 2, "s"),
+    ("spread_bias",),
+    ("load_wcs", 0, "s"),
+    ("load_wc",),
+    ("widen", 0, 1, "v"),
+    ("widen", 0, 3, "v"),
+    ("turn_s", 0),
+    ("load_wcs", 1, "g"),
+    ("widen", 0, 0, "s"),
+    ("turn_h", 0, 0),
+    ("load_h", 1, 0),
+    ("load_wo",),
+    ("widen", 0, 2, "v"),
+    ("empty_bias",),
+    ("empty_s", 0, "s"),
+    ("load_wos", 1, "y"),
+    ("turn_h", 0, 1),
+    ("permute_words",),
+    ("repeat_gain",),
+    ("load_s", 1),
+    ("quant_s", 0),
+    ("generate", 0, 0),
+    ("widen", 1, 0, "v"),
+    ("generate", 0, 1),
+    ("load_wcs", 3, "y"),
+    ("load_wcs", 2, "y"),
+    ("permute_scales",),
+    ("generate", 1, 0),
+    ("empty_h", 0, 0, "s"),
+    ("quant_h", 0, 0),
+    ("empty_h", 0, 1, "s"),
+    ("add_bias", 0, 0),
+    ("load_h", 1, 1),
+    ("project", 0, 1),
+    ("add_bias", 0, 1),
+    ("quant_h", 0, 1),
+    ("widen", 1, 1, "s"),
+    ("widen", 1, 3, "s"),
+    ("project", 0, 0),
+    ("turn_h", 1, 0),
+    ("min_gen", 0),
+    ("squash", 0, 1),
+    ("squash", 0, 0),
+    ("widen", 1, 2, "s"),
+    ("project", 0, 2),
+    ("gain", 0, 1, "v"),
+    ("project", 0, 3),
+    ("squash", 0, 2),
+    ("gain", 0, 0, "v"),
+    ("turn_s", 1),
+    ("add_bias", 1, 0),
+    ("gain", 0, 2, "v"),
+    ("turn_h", 1, 1),
+    ("squash", 0, 3),
+    ("generate", 1, 1),
+    ("gain", 0, 3, "v"),
+    ("empty_h", 1, 0, "s"),
+    ("quant_k", 0, 0),
+    ("quant_k", 0, 1),
+    ("quant_h", 1, 0),
+    ("add_bias", 1, 1),
+    ("empty_s", 1, "s"),
+    ("copy_scores", 0),
+    ("project", 1, 0),
+    ("empty_h", 1, 1, "s"),
+    ("exp_gen", 0),
+    ("squash", 1, 0),
+    ("quant_h", 1, 1),
+    ("empty_copy", 0),
+    ("project", 1, 1),
+    ("quant_s", 1),
+    ("exp_copy", 0),
+    ("min_gen", 1),
+    ("squash", 1, 1),
+    ("join", 0),
+    ("project", 1, 2),
+    ("exp_gen", 1),
+    ("generate", 2, 1),
+    ("add_bias", 2, 1),
+    ("project", 1, 3),
+    ("copy_scores", 1),
+    ("generate", 2, 0),
+    ("squash", 1, 3),
+    ("log_a", 0),
+    ("gain", 1, 1, "v"),
+    ("log_b", 0),
+    ("empty_copy", 1),
+    ("generate", 3, 1),
+    ("add_bias", 2, 0),
+    ("exp_copy", 1),
+    ("log_c", 0),
+    ("gain", 1, 0, "v"),
+    ("finish", 0, 2, "s"),
+    ("squash", 1, 2),
+    ("join", 1),
+    ("min_gen", 2),
+    ("generate", 3, 0),
+    ("log_a", 1),
+    ("finish", 0, 1, "s"),
+    ("finish", 0, 0, "g"),
+    ("exp_gen", 2),
+    ("gain", 1, 2, "v"),
+    ("log_b", 1),
+    ("gain", 1, 3, "v"),
+    ("store", 0, 2),
+    ("quant_k", 1, 0),
+    ("log_c", 1),
+    ("quant_k", 1, 1),
+    ("store", 0, 0),
+    ("copy_scores", 2),
+    ("copy_scores", 3),
+    ("finish", 1, 0, "s"),
+    ("add_bias", 3, 0),
+    ("add_bias", 3, 1),
+    ("store", 0, 1),
+    ("finish", 1, 2, "s"),
+    ("empty_copy", 2),
+    ("exp_copy", 2),
+    ("min_gen", 3),
+    ("store", 1, 0),
+    ("join", 2),
+    ("exp_gen", 3),
+    ("log_a", 2),
+    ("empty_copy", 3),
+    ("exp_copy", 3),
+    ("log_b", 2),
+    ("log_c", 2),
+    ("finish", 1, 1, "g"),
+    ("finish", 2, 1, "v"),
+    ("join", 3),
+    ("log_a", 3),
+    ("store", 1, 1),
+    ("finish", 2, 2, "s"),
+    ("log_b", 3),
+    ("finish", 2, 0, "s"),
+    ("store", 1, 2),
+    ("log_c", 3),
+    ("store", 2, 1),
+    ("finish", 3, 0, "v"),
+    ("finish", 3, 1, "g"),
+    ("store", 2, 2),
+    ("store", 2, 0),
+    ("finish", 3, 2, "s"),
+    ("store", 3, 0),
+    ("store", 3, 2),
+    ("store", 3, 1),
+)
+
+
+def tile_copynetjointgeneratecopyloglift_d2p_kernel(
+    tc, h_bytes, h_scale, wc_words, wc_scales, g, s, wo_words, wo_scales, bo, out
+):
+    nc = tc.nc
+    with ExitStack() as ctx:
+        keep = ctx.enter_context(tc.tile_pool(name="keep", bufs=1))
+        psum = ctx.enter_context(tc.psum_pool(name="psum", bufs=1))
+        ctx.enter_context(tc.manual_schedule())
+
+        def sb(name, shape, dtype):
+            return keep.tile(shape, dtype, name=name, align_bytes=64)
+
+        used = []
+
+        def bank(shape, dtype):
+            used.append(len(used) % 8)
+            return psum.tile(shape, dtype, name="bank%d" % used[-1])
+
+        ident = sb("ident", [P, P], F32)
+        minus_ones = sb("minus_ones", [P, P], BF16)
+        hs = sb("hs", [P, 32], F32)
+        hraw = [sb("hraw%d" % b, [P, 4, D], U8) for b in range(B)]
+        hwide = [sb("hwide%d" % i, [P, D], BF16) for i in range(8)]
+        hgrp = [sb("hgrp%d" % b, [P, T * PACK], BF16) for b in range(B)]
+        hq = [sb("hq%d" % b, [P, T], U32) for b in range(B)]
+        hqs = [sb("hqs%d" % b, [P, T], U8) for b in range(B)]
+        sraw = [sb("sraw%d" % b, [P, 2, D], BF16) for b in range(B)]
+        sgrp = [sb("sgrp%d" % b, [P, S * PACK], BF16) for b in range(B)]
+        sq = [sb("sq%d" % b, [P, S], U32) for b in range(B)]
+        sqs = [sb("sqs%d" % b, [P, S], U8) for b in range(B)]
+        wc_raw = sb("wc_raw", [P, 2 * D], U8)
+        wcs_raw = sb("wcs_raw", [P, D], U8)
+        wc = sb("wc", [P, 2 * D], U8)
+        wcs = sb("wcs", [P, D], U8)
+        wo = sb("wo", [P, 2 * V], U8)
+        wos = sb("wos", [P, V], U8)
+        bo_row = sb("bo_row", [P, V], BF16)
+        nbias = sb("nbias", [P, V], BF16)
+        g4 = sb("g4", [P, PACK], BF16)
+        grep = sb("grep", [P, P, PACK], BF16)
+        series = sb("series", [P, 4, 32], F32)
+        th = [sb("th%d" % i, [P, BANK], F32) for i in range(8)]
+        kgrp = [sb("kgrp%d" % b, [P, T * PACK], BF16) for b in range(B)]
+        kq = [sb("kq%d" % b, [P, T], U32) for b in range(B)]
+        kqs = [sb("kqs%d" % b, [P, T], U8) for b in range(B)]
+        nz = [sb("nz%d" % i, [P, Z], F32) for i in range(4)]
+        res = [sb("res%d" % i, [P, Z], F32) for i in range(4)]
+        ngen = [sb("ngen%d" % i, [P, 1], F32) for i in range(4)]
+        sgen = [sb("sgen%d" % i, [P, 1], F32) for i in range(4)]
+        scopy = [sb("scopy%d" % i, [P, 1], F32) for i in range(4)]
+        rescale = [sb("rescale%d" % i, [P, 1], F32) for i in range(4)]
+        total = [sb("total%d" % i, [P, 1], F32) for i in range(4)]
+        ebits = [sb("ebits%d" % i, [P, 1], I32) for i in range(4)]
+        addend = sb("addend", [P, 4, NCOL], F32)
+        factor = sb("factor", [P, 4, NCOL], F32)
+        horner = [sb("horner%d" % i, [P, NCOL], F32) for i in range(4)]
+        banks = {}
+
+        def zero(which):
+            nc.vector.memset(dict(wcs=wcs_raw, wos=wos, bo=bo_row)[which][:].bitcast(I32), 0)
+
+        def identity():
+            make_identity(nc, ident[:])
+
+        def constants():
+            nc.vector.memset(factor[:], 1.0)
+            nc.vector.memset(minus_ones[:], -1.0)
+
+        def constant_term():
+            nc.scalar.activation(out=addend[:, :, TERMS], in_=factor[:, :, NCOL - 1], func=ACT.Copy, scale=math.log(Z / CENTRE))
+
+        def coefficients():
+            nc.vector.memset(series[:, 0, 0:TERMS], -1.0)
+            nc.vector.memset(series[:, 1, 0:TERMS], -CENTRE)
+            nc.vector.tensor_tensor_scan(
+                out=series[:, 2, 0:TERMS], data0=factor[:, 0, 0:TERMS], data1=series[:, 0, 0:TERMS], initial=TERMS + 1.0, op0=ALU.mult, op1=ALU.add
+            )
+            nc.vector.tensor_tensor_scan(
+                out=series[:, 3, 0:TERMS], data0=series[:, 1, 0:TERMS], data1=factor[:, 0, 0:TERMS], initial=(-1.0 / CENTRE) ** (TERMS + 1), op0=ALU.mult, op1=ALU.mult
+            )
+            nc.vector.reciprocal(out=series[:, 0, 0:TERMS], in_=series[:, 2, 0:TERMS])
+            nc.vector.tensor_tensor(
+                out=addend[:, :, 0:TERMS], in0=series[:, 0:1, 0:TERMS].to_broadcast([P, 4, TERMS]),
+                in1=series[:, 3:4, 0:TERMS].to_broadcast([P, 4, TERMS]), op=ALU.mult,
+            )
+
+        queues = dict(y=nc.sync, s=nc.scalar, g=nc.gpsimd)
+
+        def load_hs(eng):
+            queues[eng].dma_start(out=hs[:], in_=h_scale.rearrange("b i j -> (b i j)").partition_broadcast(P))
+
+        def load_h(b, half):
+            i = slice(2 * half, 2 * half + 2)
+            nc.sync.dma_start(out=hraw[b][:, i, :], in_=h_bytes[b].rearrange("(i p) d -> p i d", p=P)[:, i, :])
+
+        def load_s(b):
+            nc.sync.dma_start(out=sraw[b][:], in_=s[b].rearrange("(p q) d -> p q d", q=2))
+
+        def load_wc():
+            nc.sync.dma_start(out=wc_raw[:].bitcast(I32), in_=wc_words[0].bitcast(I32))
+
+        def load_wo():
+            nc.sync.dma_start(out=wo[:].bitcast(I32), in_=wo_words[0].bitcast(I32))
+
+        def load_wcs(q, eng):
+            queues[eng].dma_start(out=wcs_raw[32 * q : 32 * q + 4, :].bitcast(I32), in_=wc_scales[0, 4 * q : 4 * q + 4, :].bitcast(I32))
+
+        def load_wos(q, eng):
+            queues[eng].dma_start(out=wos[32 * q : 32 * q + 4, :].bitcast(I32), in_=wo_scales[0, 4 * q : 4 * q + 4, :].bitcast(I32))
+
+        def load_bo(eng):
+            queues[eng].dma_start(out=bo_row[0:1, :], in_=bo.rearrange("(o v) -> o v", o=1))
+
+        def load_g(eng):
+            queues[eng].dma_start(out=g4[:], in_=g.rearrange("(p t) -> p t", t=PACK))
+
+        def widen(b, i, eng):
+            for j in range(4):
+                col = 16 * b + 4 * i + j
+                src = hraw[b][:, i, P * j : P * (j + 1)].bitcast(FP8)
+                dst = hwide[4 * b + i][:, P * j : P * (j + 1)]
+                if eng == "s":
+                    nc.scalar.activation(out=dst, in_=src, func=ACT.Copy, scale=hs[:, col : col + 1])
+                else:
+                    nc.vector.tensor_scalar(out=dst, in0=src, scalar1=hs[:, col : col + 1], scalar2=None, op0=ALU.mult)
+
+        def turn(key, slot, rows):
+            if key not in banks:
+                banks[key] = bank([P, 2, 2, P], F32)
+            words = rows.bitcast(F32)
+            for u in range(2):
+                nc.tensor.transpose(banks[key][:, slot, u, :], words[:, u : D // 2 : 2], ident[:])
+
+        def empty_turned(key, dst, eng):
+            words = dst.bitcast(F32).rearrange("p (i r u) -> p i r u", i=2, u=2)
+            turned = banks[key][:].rearrange("p i u r -> p i r u")
+            if eng == "s":
+                nc.scalar.copy(out=words, in_=turned)
+            else:
+                nc.vector.tensor_copy(out=words, in_=turned)
+
+        def turn_h(b, half):
+            for slot in range(2):
+                turn(("h", b, half), slot, hwide[4 * b + 2 * half + slot][:])
+
+        def empty_h(b, half, eng):
+            empty_turned(("h", b, half), hgrp[b][:, 1024 * half : 1024 * (half + 1)], eng)
+
+        def turn_s(b):
+            for q in range(2):
+                turn(("s", b), q, sraw[b][:, q, :])
+
+        def empty_s(b, eng):
+            empty_turned(("s", b), sgrp[b][:], eng)
+
+        def quant(codes, scales, src):
+            nc.vector.quantize_mx(out=codes.bitcast(FP8X4), scales=scales, in_=src)
+
+        def quant_h(b, half):
+            c = slice(256 * half, 256 * (half + 1))
+            quant(hq[b][:, c], hqs[b][:, c], hgrp[b][:, 1024 * half : 1024 * (half + 1)])
+
+        def quant_k(b, half):
+            c = slice(256 * half, 256 * (half + 1))
+            quant(kq[b][:, c], kqs[b][:, c], kgrp[b][:, 1024 * half : 1024 * (half + 1)])
+
+        def project(b, c):
+            banks["p", b, c] = bank([P, PACK, P], F32)
+            cols = slice(P * c, P * (c + 1))
+            for t in range(PACK):
+                nc.tensor.matmul_mx(
+                    out=banks["p", b, c][:, t, :],
+                    lhsT=wc[:, 2 * P * t : 2 * P * (t + 1)].bitcast(FP4X4),
+                    lhsT_scale=wcs[:, P * t : P * (t + 1)],
+                    rhs=hq[b][:, cols].bitcast(FP8X4),
+                    rhs_scale=hqs[b][:, cols],
+                    start=True,
+                    stop=True,
+                )
+
+        def squash(b, c):
+            nc.scalar.activation(
+                out=th[4 * b + c][:].rearrange("p (n t) -> p n t", t=PACK),
+                in_=banks["p", b, c][:].rearrange("p t n -> p n t"),
+                func=ACT.Tanh,
+            )
+
+        def gain(b, c, eng):
+            (nc.gpsimd if eng == "g" else nc.vector).tensor_tensor(
+                out=kgrp[b][:, BANK * c : BANK * (c + 1)],
+                in0=th[4 * b + c][:],
+                in1=grep[:].rearrange("p n t -> p (n t)"),
+                op=ALU.mult,
+            )
+
+        def generate(n, half):
+            b, q = divmod(n, 2)
+            rows = slice(P * q, P * (q + 1))
+            banks["g", n, half] = bank([P, BANK], F32)
+            nc.tensor.matmul_mx(
+                out=banks["g", n, half][:],
+                lhsT=sq[b][:, rows].bitcast(FP8X4),
+                lhsT_scale=sqs[b][:, rows],
+                rhs=wo[:, 2 * BANK * half : 2 * BANK * (half + 1)].bitcast(FP4X4),
+                rhs_scale=wos[:, BANK * half : BANK * (half + 1)],
+                start=True,
+                stop=True,
+            )
+
+        def add_bias(n, half):
+            c = slice(BANK * half, BANK * (half + 1))
+            nc.vector.tensor_tensor(out=nz[n][:, c], in0=nbias[:, c], in1=banks["g", n, half][:], op=ALU.subtract)
+
+        def min_gen(n):
+            nc.vector.tensor_reduce(out=ngen[n][:], in_=nz[n][:, 0:V], axis=AX.X, op=ALU.min)
+
+        def copy_scores(n):
+            b, q = divmod(n, 2)
+            rows = slice(P * q, P * (q + 1))
+            banks["c", n] = bank([P, BANK], F32)
+            nc.tensor.matmul_mx(
+                out=banks["c", n][:],
+                lhsT=sq[b][:, rows].bitcast(FP8X4),
+                lhsT_scale=sqs[b][:, rows],
+                rhs=kq[b][:].bitcast(FP8X4),
+                rhs_scale=kqs[b][:],
+                start=True,
+                stop=True,
+            )
+
+        def empty_copy(n):
+            nc.vector.tensor_scalar(
+                out=nz[n][:, V:Z],
+                in0=banks["c", n][:],
+                scalar1=-1.0 / math.sqrt(D),
+                scalar2=ngen[n][:],
+                op0=ALU.mult,
+                op1=ALU.min,
+                accum_out=addend[:, n, NCOL - 1 : NCOL],
+            )
+
+        def exp_gen(n):
+            nc.scalar.activation(
+                out=res[n][:, 0:V], in_=nz[n][:, 0:V], func=ACT.Exp, scale=-1.0, bias=ngen[n][:], accum_out=sgen[n][:]
+            )
+
+        def exp_copy(n):
+            shift = addend[:, n, NCOL - 1 : NCOL]
+            nc.scalar.activation(out=rescale[n][:], in_=ngen[n][:], func=ACT.Exp, scale=-1.0, bias=shift)
+            nc.scalar.activation(out=res[n][:, V:Z], in_=nz[n][:, V:Z], func=ACT.Exp, scale=-1.0, bias=shift, accum_out=scopy[n][:])
+
+        def join(n):
+            nc.vector.tensor_scalar(
+                out=total[n][:], in0=sgen[n][:], scalar1=rescale[n][:], scalar2=scopy[n][:], op0=ALU.mult, op1=ALU.add
+            )
+
+        def log_a(n):
+            nc.vector.tensor_scalar(
+                out=ebits[n][:], in0=total[n][:].bitcast(I32), scalar1=EXP_MASK, scalar2=EXP_MASK,
+                op0=ALU.bitwise_xor, op1=ALU.bitwise_and,
+            )
+
+        def log_b(n):
+            nc.vector.tensor_scalar(
+                out=factor[:, n, 0 : TERMS + 1], in0=ebits[n][:].bitcast(F32).to_broadcast([P, TERMS + 1]),
+                scalar1=total[n][:], scalar2=-CENTRE, op0=ALU.mult, op1=ALU.add,
+            )
+            nc.vector.tensor_scalar(
+                out=addend[:, n, TERMS + 1 : TERMS + 2], in0=ebits[n][:],
+                scalar1=-127.0 * 2.0**23, scalar2=math.log(2.0) / 2.0**23, op0=ALU.add, op1=ALU.mult,
+            )
+
+        def log_c(n):
+            nc.vector.tensor_tensor_scan(
+                out=horner[n][:], data0=factor[:, n, :], data1=addend[:, n, :], initial=0.0, op0=ALU.mult, op1=ALU.add
+            )
+
+        def finish(n, part, eng):
+            c0, c1 = BANK * part, BANK * (part + 1)
+            shift = horner[n][:, NCOL - 1 : NCOL]
+            if eng == "s":
+                nc.scalar.activation(out=res[n][:, c0:c1], in_=nz[n][:, c0:c1], func=ACT.Identity, scale=-1.0, bias=shift)
+            else:
+                e = nc.gpsimd if eng == "g" else nc.vector
+                e.tensor_scalar(out=res[n][:, c0:c1], in0=nz[n][:, c0:c1], scalar1=-1.0, scalar2=shift, op0=ALU.mult, op1=ALU.add)
+
+        def store(n, part):
+            b, q = divmod(n, 2)
+            c0, c1 = BANK * part, BANK * (part + 1)
+            nc.sync.dma_start(out=out[b].rearrange("(p q) v -> q p v", q=2)[q][:, c0:c1], in_=res[n][:, c0:c1])
+
+        def permute_words():
+            nc.vector.tensor_copy(
+                out=wc[:].rearrange("p (t m e) -> p t m e", t=PACK, e=2), in_=wc_raw[:].rearrange("p (m t e) -> p t m e", t=PACK, e=2)
+            )
+
+        def permute_scales():
+            nc.vector.tensor_copy(
+                out=wcs[:].rearrange("p (t m) -> p t m", t=PACK), in_=wcs_raw[:].rearrange("p (m t) -> p t m", t=PACK)
+            )
+
+        def spread_bias():
+            banks["bias"] = bank([P, V], BF16)
+            for half in range(2):
+                c = slice(BANK * half, BANK * (half + 1))
+                nc.tensor.matmul(out=banks["bias"][:, c], lhsT=minus_ones[:], rhs=bo_row[:, c], start=True, stop=True)
+
+        def empty_bias():
+            nc.scalar.copy(out=nbias[:], in_=banks["bias"][:])
+
+        def repeat_gain():
+            nc.vector.tensor_copy(out=grep[:], in_=g4[:].unsqueeze(1).to_broadcast([P, P, PACK]))
+
+        def quant_s(b):
+            quant(sq[b][:], sqs[b][:], sgrp[b][:])
+
+        steps = dict(
+            widen=widen, turn_h=turn_h, turn_s=turn_s, empty_h=empty_h, empty_s=empty_s, quant_h=quant_h, quant_s=quant_s,
+            quant_k=quant_k, project=project, squash=squash, gain=gain, generate=generate, add_bias=add_bias, min_gen=min_gen,
+            copy_scores=copy_scores, empty_copy=empty_copy, exp_gen=exp_gen, exp_copy=exp_copy, join=join, store=store, load_hs=load_hs, load_h=load_h, load_s=load_s,
+            load_wc=load_wc, load_wo=load_wo, load_wcs=load_wcs, load_wos=load_wos, load_bo=load_bo, load_g=load_g, log_a=log_a, log_b=log_b, log_c=log_c, finish=finish,
+            permute_words=permute_words, permute_scales=permute_scales, spread_bias=spread_bias, empty_bias=empty_bias,
+            repeat_gain=repeat_gain, zero=zero, identity=identity, constants=constants, constant_term=constant_term,
+            coefficients=coefficients,
+        )
+        for name, *args in ORDER:
+            steps[name](*args)

@@ -29,167 +29,178 @@ EXP_MASK = 0x7F800000
 NCOL = TERMS + 3
 
 ORDER = (
-    ("load_s", 0),
-    ("load_h", 0, 0),
-    ("zero", "bo"),
-    ("load_bo", "y"),
+    ("zero", "g"),
+    ("load_s", 0, 0, 1),
     ("zero", "wcs"),
-    ("constants",),
+    ("load_g", "s"),
+    ("zero", "ident"),
     ("load_hs", "y"),
-    ("load_h", 0, 1),
-    ("zero", "wos"),
-    ("load_g", "y"),
-    ("load_wos", 3, "g"),
+    ("load_wcs", 2, "g"),
+    ("constants",),
     ("constant_term",),
+    ("load_h", 0, 0, 2),
+    ("zero", "bo"),
+    ("load_h", 0, 2, 2),
+    ("load_bo", "y"),
     ("identity",),
-    ("coefficients",),
-    ("load_wos", 0, "y"),
-    ("load_wos", 2, "s"),
-    ("spread_bias",),
-    ("load_wcs", 0, "s"),
-    ("load_wc",),
-    ("widen", 0, 1, "v"),
-    ("widen", 0, 3, "v"),
-    ("turn_s", 0),
-    ("load_wcs", 1, "g"),
-    ("widen", 0, 0, "s"),
-    ("turn_h", 0, 0),
-    ("load_h", 1, 0),
-    ("load_wo",),
-    ("widen", 0, 2, "v"),
-    ("empty_bias",),
-    ("empty_s", 0, "s"),
-    ("load_wos", 1, "y"),
-    ("turn_h", 0, 1),
-    ("permute_words",),
+    ("widen", 0, 1, "s"),
+    ("load_wcs", 3, "g"),
+    ("turn_s", 0, 0),
+    ("zero", "wos"),
     ("repeat_gain",),
-    ("load_s", 1),
-    ("quant_s", 0),
-    ("generate", 0, 0),
-    ("widen", 1, 0, "v"),
-    ("generate", 0, 1),
-    ("load_wcs", 3, "y"),
-    ("load_wcs", 2, "y"),
-    ("permute_scales",),
-    ("generate", 1, 0),
+    ("load_wc",),
+    ("coefficients",),
+    ("load_wos", 3, "s"),
+    ("empty_s", 0, 0, "v"),
+    ("widen", 0, 0, "v"),
+    ("widen", 0, 3, "v"),
+    ("spread_bias",),
+    ("load_wcs", 1, "s"),
+    ("load_h", 1, 0, 4),
+    ("permute_words",),
+    ("load_wos", 0, "y"),
+    ("widen", 1, 3, "v"),
+    ("load_s", 0, 1, 1),
+    ("load_wcs", 0, "y"),
+    ("load_wos", 2, "g"),
+    ("load_s", 1, 0, 2),
+    ("widen", 1, 1, "v"),
+    ("load_wo", 1),
+    ("widen", 0, 2, "s"),
+    ("load_wo", 0),
+    ("quant_s", 0, 0),
+    ("turn_h", 0, 0),
+    ("empty_bias",),
     ("empty_h", 0, 0, "s"),
-    ("quant_h", 0, 0),
+    ("turn_h", 0, 1),
+    ("load_wos", 1, "g"),
+    ("turn_s", 0, 1),
+    ("turn_s", 1, 0),
     ("empty_h", 0, 1, "s"),
-    ("add_bias", 0, 0),
-    ("load_h", 1, 1),
-    ("project", 0, 1),
-    ("add_bias", 0, 1),
+    ("permute_scales",),
+    ("generate", 0, 1),
+    ("quant_h", 0, 0),
+    ("generate", 0, 0),
+    ("empty_s", 0, 1, "s"),
     ("quant_h", 0, 1),
-    ("widen", 1, 1, "s"),
-    ("widen", 1, 3, "s"),
-    ("project", 0, 0),
-    ("turn_h", 1, 0),
-    ("min_gen", 0),
-    ("squash", 0, 1),
-    ("squash", 0, 0),
+    ("project", 0, 1),
+    ("empty_s", 1, 0, "s"),
     ("widen", 1, 2, "s"),
-    ("project", 0, 2),
-    ("gain", 0, 1, "v"),
     ("project", 0, 3),
-    ("squash", 0, 2),
-    ("gain", 0, 0, "v"),
-    ("turn_s", 1),
-    ("add_bias", 1, 0),
-    ("gain", 0, 2, "v"),
+    ("project", 0, 2),
+    ("quant_s", 0, 1),
+    ("project", 0, 0),
+    ("widen", 1, 0, "s"),
+    ("empty_gen", 0, 1, "v"),
+    ("turn_h", 1, 0),
     ("turn_h", 1, 1),
-    ("squash", 0, 3),
+    ("empty_gen", 0, 0, "v"),
     ("generate", 1, 1),
-    ("gain", 0, 3, "v"),
-    ("empty_h", 1, 0, "s"),
-    ("quant_k", 0, 0),
-    ("quant_k", 0, 1),
-    ("quant_h", 1, 0),
-    ("add_bias", 1, 1),
-    ("empty_s", 1, "s"),
-    ("copy_scores", 0),
-    ("project", 1, 0),
-    ("empty_h", 1, 1, "s"),
-    ("exp_gen", 0),
-    ("squash", 1, 0),
-    ("quant_h", 1, 1),
-    ("empty_copy", 0),
-    ("project", 1, 1),
-    ("quant_s", 1),
-    ("exp_copy", 0),
-    ("min_gen", 1),
-    ("squash", 1, 1),
-    ("join", 0),
-    ("project", 1, 2),
-    ("exp_gen", 1),
-    ("generate", 2, 1),
-    ("add_bias", 2, 1),
-    ("project", 1, 3),
-    ("copy_scores", 1),
+    ("empty_gain",),
+    ("squash", 0, 1),
+    ("squash", 0, 3),
+    ("squash", 0, 2),
+    ("quant_s", 1, 0),
+    ("gain", 0, 3, "g"),
     ("generate", 2, 0),
+    ("squash", 0, 0),
+    ("empty_h", 1, 0, "s"),
+    ("empty_h", 1, 1, "s"),
+    ("min_gen", 0),
+    ("gain", 0, 1, "v"),
+    ("gain", 0, 2, "v"),
+    ("gain", 0, 0, "v"),
+    ("quant_h", 1, 0),
+    ("quant_k", 0, 1),
+    ("empty_gen", 1, 1, "s"),
+    ("quant_k", 0, 0),
+    ("generate", 1, 0),
+    ("generate", 2, 1),
+    ("quant_h", 1, 1),
+    ("copy_scores", 0),
+    ("exp_gen", 0),
+    ("empty_gen", 1, 0, "v"),
+    ("project", 1, 3),
+    ("empty_gen", 2, 0, "v"),
     ("squash", 1, 3),
-    ("log_a", 0),
-    ("gain", 1, 1, "v"),
-    ("log_b", 0),
-    ("empty_copy", 1),
-    ("generate", 3, 1),
-    ("add_bias", 2, 0),
-    ("exp_copy", 1),
-    ("log_c", 0),
+    ("empty_gen", 2, 1, "v"),
+    ("project", 1, 0),
+    ("add_bias", 1, 1),
+    ("turn_s", 1, 1),
+    ("empty_copy", 0),
+    ("project", 1, 2),
+    ("min_gen", 1),
+    ("gain", 1, 3, "g"),
+    ("squash", 1, 0),
     ("gain", 1, 0, "v"),
-    ("finish", 0, 2, "s"),
+    ("empty_s", 1, 1, "s"),
+    ("exp_copy", 0),
+    ("join", 0),
+    ("project", 1, 1),
+    ("quant_s", 1, 1),
     ("squash", 1, 2),
-    ("join", 1),
+    ("copy_scores", 1),
+    ("empty_copy", 1),
     ("min_gen", 2),
     ("generate", 3, 0),
-    ("log_a", 1),
-    ("finish", 0, 1, "s"),
-    ("finish", 0, 0, "g"),
-    ("exp_gen", 2),
-    ("gain", 1, 2, "v"),
-    ("log_b", 1),
-    ("gain", 1, 3, "v"),
-    ("store", 0, 2),
-    ("quant_k", 1, 0),
-    ("log_c", 1),
+    ("squash", 1, 1),
+    ("exp_gen", 1),
+    ("log_a", 0),
+    ("exp_copy", 1),
+    ("gain", 1, 1, "v"),
+    ("gain", 1, 2, "g"),
+    ("log_b", 0),
+    ("join", 1),
     ("quant_k", 1, 1),
-    ("store", 0, 0),
-    ("copy_scores", 2),
-    ("copy_scores", 3),
+    ("log_c", 0),
+    ("exp_gen", 2),
+    ("log_a", 1),
+    ("quant_k", 1, 0),
+    ("log_b", 1),
+    ("finish", 0, 2, "s"),
+    ("generate", 3, 1),
+    ("empty_gen", 3, 0, "v"),
+    ("log_c", 1),
+    ("finish", 0, 0, "s"),
     ("finish", 1, 0, "s"),
-    ("add_bias", 3, 0),
-    ("add_bias", 3, 1),
-    ("store", 0, 1),
-    ("finish", 1, 2, "s"),
+    ("finish", 1, 1, "s"),
+    ("store", 0, 2),
+    ("empty_gen", 3, 1, "v"),
+    ("store", 0, 0),
+    ("store", 1, 0),
+    ("store", 1, 1),
+    ("copy_scores", 2),
     ("empty_copy", 2),
     ("exp_copy", 2),
     ("min_gen", 3),
-    ("store", 1, 0),
     ("join", 2),
-    ("exp_gen", 3),
+    ("copy_scores", 3),
     ("log_a", 2),
-    ("empty_copy", 3),
-    ("exp_copy", 3),
-    ("log_b", 2),
-    ("log_c", 2),
-    ("finish", 1, 1, "g"),
-    ("finish", 2, 1, "v"),
-    ("join", 3),
-    ("log_a", 3),
-    ("store", 1, 1),
-    ("finish", 2, 2, "s"),
-    ("log_b", 3),
-    ("finish", 2, 0, "s"),
+    ("finish", 1, 2, "g"),
     ("store", 1, 2),
+    ("empty_copy", 3),
+    ("log_b", 2),
+    ("finish", 0, 1, "g"),
+    ("log_c", 2),
+    ("exp_gen", 3),
+    ("finish", 2, 1, "v"),
+    ("exp_copy", 3),
+    ("store", 0, 1),
+    ("join", 3),
+    ("finish", 2, 2, "s"),
+    ("log_a", 3),
+    ("log_b", 3),
     ("log_c", 3),
-    ("store", 2, 1),
     ("finish", 3, 0, "v"),
-    ("finish", 3, 1, "g"),
+    ("store", 2, 1),
+    ("finish", 2, 0, "s"),
+    ("finish", 3, 1, "s"),
     ("store", 2, 2),
     ("store", 2, 0),
-    ("finish", 3, 2, "s"),
     ("store", 3, 0),
-    ("store", 3, 2),
     ("store", 3, 1),
+    ("finish", 3, 2, "s"),
+    ("store", 3, 2),
 )
 
 
@@ -205,11 +216,16 @@ def tile_copynetjointgeneratecopyloglift_d2p_kernel(
         def sb(name, shape, dtype):
             return keep.tile(shape, dtype, name=name, align_bytes=64)
 
-        used = []
+        free = list(range(8))
+        held = {}
 
-        def bank(shape, dtype):
-            used.append(len(used) % 8)
-            return psum.tile(shape, dtype, name="bank%d" % used[-1])
+        def bank(key, shape, dtype):
+            held[key] = free[0]
+            free.remove(held[key])
+            banks[key] = psum.tile(shape, dtype, name="bank%d" % held[key])
+
+        def release(key):
+            free.append(held[key])
 
         ident = sb("ident", [P, P], F32)
         minus_ones = sb("minus_ones", [P, P], BF16)
@@ -231,8 +247,9 @@ def tile_copynetjointgeneratecopyloglift_d2p_kernel(
         wos = sb("wos", [P, V], U8)
         bo_row = sb("bo_row", [P, V], BF16)
         nbias = sb("nbias", [P, V], BF16)
-        g4 = sb("g4", [P, PACK], BF16)
-        grep = sb("grep", [P, P, PACK], BF16)
+        g4 = sb("g4", [P, PACK], F32)
+        g_row = sb("g_row", [P, D], BF16)
+        ones = sb("ones", [P, P], BF16)
         series = sb("series", [P, 4, 32], F32)
         th = [sb("th%d" % i, [P, BANK], F32) for i in range(8)]
         kgrp = [sb("kgrp%d" % b, [P, T * PACK], BF16) for b in range(B)]
@@ -252,14 +269,15 @@ def tile_copynetjointgeneratecopyloglift_d2p_kernel(
         banks = {}
 
         def zero(which):
-            nc.vector.memset(dict(wcs=wcs_raw, wos=wos, bo=bo_row)[which][:].bitcast(I32), 0)
+            nc.vector.memset(dict(wcs=wcs_raw, wos=wos, bo=bo_row, g=g_row, ident=ident)[which][:].bitcast(I32), 0)
 
         def identity():
-            make_identity(nc, ident[:])
+            make_identity(nc, ident[:], nomemset=True)
 
         def constants():
             nc.vector.memset(factor[:], 1.0)
             nc.vector.memset(minus_ones[:], -1.0)
+            nc.vector.memset(ones[:], 1.0)
 
         def constant_term():
             nc.scalar.activation(out=addend[:, :, TERMS], in_=factor[:, :, NCOL - 1], func=ACT.Copy, scale=math.log(Z / CENTRE))
@@ -284,18 +302,20 @@ def tile_copynetjointgeneratecopyloglift_d2p_kernel(
         def load_hs(eng):
             queues[eng].dma_start(out=hs[:], in_=h_scale.rearrange("b i j -> (b i j)").partition_broadcast(P))
 
-        def load_h(b, half):
-            i = slice(2 * half, 2 * half + 2)
+        def load_h(b, first, count):
+            i = slice(first, first + count)
             nc.sync.dma_start(out=hraw[b][:, i, :], in_=h_bytes[b].rearrange("(i p) d -> p i d", p=P)[:, i, :])
 
-        def load_s(b):
-            nc.sync.dma_start(out=sraw[b][:], in_=s[b].rearrange("(p q) d -> p q d", q=2))
+        def load_s(b, first, count):
+            q = slice(first, first + count)
+            nc.sync.dma_start(out=sraw[b][:, q, :], in_=s[b].rearrange("(q p) d -> p q d", p=P)[:, q, :])
 
         def load_wc():
             nc.sync.dma_start(out=wc_raw[:].bitcast(I32), in_=wc_words[0].bitcast(I32))
 
-        def load_wo():
-            nc.sync.dma_start(out=wo[:].bitcast(I32), in_=wo_words[0].bitcast(I32))
+        def load_wo(half):
+            c = slice(2 * BANK * half, 2 * BANK * (half + 1))
+            nc.sync.dma_start(out=wo[:, c].bitcast(I32), in_=wo_words[0][:, c].bitcast(I32))
 
         def load_wcs(q, eng):
             queues[eng].dma_start(out=wcs_raw[32 * q : 32 * q + 4, :].bitcast(I32), in_=wc_scales[0, 4 * q : 4 * q + 4, :].bitcast(I32))
@@ -307,7 +327,7 @@ def tile_copynetjointgeneratecopyloglift_d2p_kernel(
             queues[eng].dma_start(out=bo_row[0:1, :], in_=bo.rearrange("(o v) -> o v", o=1))
 
         def load_g(eng):
-            queues[eng].dma_start(out=g4[:], in_=g.rearrange("(p t) -> p t", t=PACK))
+            queues[eng].dma_start(out=g_row[0:1, :], in_=g.rearrange("(o d) -> o d", o=1))
 
         def widen(b, i, eng):
             for j in range(4):
@@ -319,34 +339,33 @@ def tile_copynetjointgeneratecopyloglift_d2p_kernel(
                 else:
                     nc.vector.tensor_scalar(out=dst, in0=src, scalar1=hs[:, col : col + 1], scalar2=None, op0=ALU.mult)
 
-        def turn(key, slot, rows):
-            if key not in banks:
-                banks[key] = bank([P, 2, 2, P], F32)
-            words = rows.bitcast(F32)
-            for u in range(2):
-                nc.tensor.transpose(banks[key][:, slot, u, :], words[:, u : D // 2 : 2], ident[:])
+        def turn(key, tiles):
+            bank(key, [P, len(tiles), 2, P], F32)
+            for slot, rows in enumerate(tiles):
+                words = rows.bitcast(F32)
+                for u in range(2):
+                    nc.tensor.transpose(banks[key][:, slot, u, :], words[:, u : D // 2 : 2], ident[:])
 
         def empty_turned(key, dst, eng):
-            words = dst.bitcast(F32).rearrange("p (i r u) -> p i r u", i=2, u=2)
+            words = dst.bitcast(F32).rearrange("p (i r u) -> p i r u", r=P, u=2)
             turned = banks[key][:].rearrange("p i u r -> p i r u")
             if eng == "s":
                 nc.scalar.copy(out=words, in_=turned)
             else:
                 nc.vector.tensor_copy(out=words, in_=turned)
+            release(key)
 
         def turn_h(b, half):
-            for slot in range(2):
-                turn(("h", b, half), slot, hwide[4 * b + 2 * half + slot][:])
+            turn(("h", b, half), [hwide[4 * b + 2 * half + slot][:] for slot in range(2)])
 
         def empty_h(b, half, eng):
             empty_turned(("h", b, half), hgrp[b][:, 1024 * half : 1024 * (half + 1)], eng)
 
-        def turn_s(b):
-            for q in range(2):
-                turn(("s", b), q, sraw[b][:, q, :])
+        def turn_s(b, q):
+            turn(("s", b, q), [sraw[b][:, q, :]])
 
-        def empty_s(b, eng):
-            empty_turned(("s", b), sgrp[b][:], eng)
+        def empty_s(b, q, eng):
+            empty_turned(("s", b, q), sgrp[b][:, BANK * q : BANK * (q + 1)], eng)
 
         def quant(codes, scales, src):
             nc.vector.quantize_mx(out=codes.bitcast(FP8X4), scales=scales, in_=src)
@@ -360,7 +379,7 @@ def tile_copynetjointgeneratecopyloglift_d2p_kernel(
             quant(kq[b][:, c], kqs[b][:, c], kgrp[b][:, 1024 * half : 1024 * (half + 1)])
 
         def project(b, c):
-            banks["p", b, c] = bank([P, PACK, P], F32)
+            bank(("p", b, c), [P, PACK, P], F32)
             cols = slice(P * c, P * (c + 1))
             for t in range(PACK):
                 nc.tensor.matmul_mx(
@@ -379,19 +398,29 @@ def tile_copynetjointgeneratecopyloglift_d2p_kernel(
                 in_=banks["p", b, c][:].rearrange("p t n -> p n t"),
                 func=ACT.Tanh,
             )
+            release(("p", b, c))
 
         def gain(b, c, eng):
-            (nc.gpsimd if eng == "g" else nc.vector).tensor_tensor(
-                out=kgrp[b][:, BANK * c : BANK * (c + 1)],
-                in0=th[4 * b + c][:],
-                in1=grep[:].rearrange("p n t -> p (n t)"),
-                op=ALU.mult,
-            )
+            dst = kgrp[b][:, BANK * c : BANK * (c + 1)]
+            if eng == "v":
+                nc.vector.tensor_tensor(
+                    out=dst, in0=th[4 * b + c][:], in1=banks["gain"][:].rearrange("p n t -> p (n t)"), op=ALU.mult
+                )
+            else:
+                nc.gpsimd.tensor_tensor(
+                    out=dst.rearrange("p (n t) -> p n t", t=PACK),
+                    in0=th[4 * b + c][:].rearrange("p (n t) -> p n t", t=PACK),
+                    in1=g4[:].unsqueeze(1).to_broadcast([P, P, PACK]),
+                    op=ALU.mult,
+                )
+
+        def empty_gain():
+            nc.vector.tensor_copy(out=g4[:], in_=banks["gain"][:, 0, :])
 
         def generate(n, half):
             b, q = divmod(n, 2)
             rows = slice(P * q, P * (q + 1))
-            banks["g", n, half] = bank([P, BANK], F32)
+            bank(("g", n, half), [P, BANK], F32)
             nc.tensor.matmul_mx(
                 out=banks["g", n, half][:],
                 lhsT=sq[b][:, rows].bitcast(FP8X4),
@@ -402,9 +431,17 @@ def tile_copynetjointgeneratecopyloglift_d2p_kernel(
                 stop=True,
             )
 
+        def empty_gen(n, half, eng):
+            c = slice(BANK * half, BANK * (half + 1))
+            if eng == "v":
+                nc.vector.tensor_tensor(out=nz[n][:, c], in0=nbias[:, c], in1=banks["g", n, half][:], op=ALU.subtract)
+            else:
+                nc.scalar.activation(out=nz[n][:, c], in_=banks["g", n, half][:], func=ACT.Copy, scale=-1.0)
+            release(("g", n, half))
+
         def add_bias(n, half):
             c = slice(BANK * half, BANK * (half + 1))
-            nc.vector.tensor_tensor(out=nz[n][:, c], in0=nbias[:, c], in1=banks["g", n, half][:], op=ALU.subtract)
+            nc.gpsimd.tensor_tensor(out=nz[n][:, c], in0=nz[n][:, c], in1=nbias[:, c], op=ALU.add)
 
         def min_gen(n):
             nc.vector.tensor_reduce(out=ngen[n][:], in_=nz[n][:, 0:V], axis=AX.X, op=ALU.min)
@@ -412,7 +449,7 @@ def tile_copynetjointgeneratecopyloglift_d2p_kernel(
         def copy_scores(n):
             b, q = divmod(n, 2)
             rows = slice(P * q, P * (q + 1))
-            banks["c", n] = bank([P, BANK], F32)
+            bank(("c", n), [P, BANK], F32)
             nc.tensor.matmul_mx(
                 out=banks["c", n][:],
                 lhsT=sq[b][:, rows].bitcast(FP8X4),
@@ -433,6 +470,7 @@ def tile_copynetjointgeneratecopyloglift_d2p_kernel(
                 op1=ALU.min,
                 accum_out=addend[:, n, NCOL - 1 : NCOL],
             )
+            release(("c", n))
 
         def exp_gen(n):
             nc.scalar.activation(
@@ -482,7 +520,7 @@ def tile_copynetjointgeneratecopyloglift_d2p_kernel(
         def store(n, part):
             b, q = divmod(n, 2)
             c0, c1 = BANK * part, BANK * (part + 1)
-            nc.sync.dma_start(out=out[b].rearrange("(p q) v -> q p v", q=2)[q][:, c0:c1], in_=res[n][:, c0:c1])
+            nc.sync.dma_start(out=out[b, P * q : P * (q + 1), c0:c1], in_=res[n][:, c0:c1])
 
         def permute_words():
             nc.vector.tensor_copy(
@@ -495,23 +533,27 @@ def tile_copynetjointgeneratecopyloglift_d2p_kernel(
             )
 
         def spread_bias():
-            banks["bias"] = bank([P, V], BF16)
+            bank("bias", [P, V], BF16)
             for half in range(2):
                 c = slice(BANK * half, BANK * (half + 1))
                 nc.tensor.matmul(out=banks["bias"][:, c], lhsT=minus_ones[:], rhs=bo_row[:, c], start=True, stop=True)
 
         def empty_bias():
             nc.scalar.copy(out=nbias[:], in_=banks["bias"][:])
+            release("bias")
 
         def repeat_gain():
-            nc.vector.tensor_copy(out=grep[:], in_=g4[:].unsqueeze(1).to_broadcast([P, P, PACK]))
+            bank("gain", [P, P, PACK], F32)
+            for t in range(PACK):
+                nc.tensor.matmul(out=banks["gain"][:, :, t], lhsT=g_row[:, t:D:PACK], rhs=ones[:], start=True, stop=True)
 
-        def quant_s(b):
-            quant(sq[b][:], sqs[b][:], sgrp[b][:])
+        def quant_s(b, q):
+            c = slice(P * q, P * (q + 1))
+            quant(sq[b][:, c], sqs[b][:, c], sgrp[b][:, BANK * q : BANK * (q + 1)])
 
         steps = dict(
             widen=widen, turn_h=turn_h, turn_s=turn_s, empty_h=empty_h, empty_s=empty_s, quant_h=quant_h, quant_s=quant_s,
-            quant_k=quant_k, project=project, squash=squash, gain=gain, generate=generate, add_bias=add_bias, min_gen=min_gen,
+            quant_k=quant_k, project=project, squash=squash, gain=gain, empty_gain=empty_gain, generate=generate, add_bias=add_bias, empty_gen=empty_gen, min_gen=min_gen,
             copy_scores=copy_scores, empty_copy=empty_copy, exp_gen=exp_gen, exp_copy=exp_copy, join=join, store=store, load_hs=load_hs, load_h=load_h, load_s=load_s,
             load_wc=load_wc, load_wo=load_wo, load_wcs=load_wcs, load_wos=load_wos, load_bo=load_bo, load_g=load_g, log_a=log_a, log_b=log_b, log_c=log_c, finish=finish,
             permute_words=permute_words, permute_scales=permute_scales, spread_bias=spread_bias, empty_bias=empty_bias,

import math
from contextlib import ExitStack

import concourse.mybir as mybir
from concourse.masks import make_identity

B, S, T, D, V = 2, 256, 512, 512, 1024
FLOPS = 2 * B * (T * D * D + S * T * D + S * D * V)

F32 = mybir.dt.float32
BF16 = mybir.dt.bfloat16
I32 = mybir.dt.int32
U32 = mybir.dt.uint32
U8 = mybir.dt.uint8
FP8 = mybir.dt.float8_e4m3fn
FP8X4 = mybir.dt.float8_e4m3fn_x4
FP4X4 = mybir.dt.float4_e2m1fn_x4
ALU = mybir.AluOpType
ACT = mybir.ActivationFunctionType
AX = mybir.AxisListType

P = 128
PACK = 4
BANK = 512
Z = V + T
TERMS = 30
CENTRE = 3.25
EXP_MASK = 0x7F800000
NCOL = TERMS + 3

ORDER = (
    ("zero", "g"),
    ("load_s", 0, 0, 1),
    ("zero", "wcs"),
    ("load_g", "s"),
    ("zero", "ident"),
    ("load_hs", "y"),
    ("load_wcs", 2, "g"),
    ("constants",),
    ("constant_term",),
    ("load_h", 0, 0, 2),
    ("zero", "bo"),
    ("load_h", 0, 2, 2),
    ("load_bo", "y"),
    ("identity",),
    ("widen", 0, 1, "s"),
    ("load_wcs", 3, "g"),
    ("turn_s", 0, 0),
    ("zero", "wos"),
    ("repeat_gain",),
    ("load_wc",),
    ("coefficients",),
    ("load_wos", 3, "s"),
    ("empty_s", 0, 0, "v"),
    ("widen", 0, 0, "v"),
    ("widen", 0, 3, "v"),
    ("spread_bias",),
    ("load_wcs", 1, "s"),
    ("load_h", 1, 0, 4),
    ("permute_words",),
    ("load_wos", 0, "y"),
    ("widen", 1, 3, "v"),
    ("load_s", 0, 1, 1),
    ("load_wcs", 0, "y"),
    ("load_wos", 2, "g"),
    ("load_s", 1, 0, 2),
    ("widen", 1, 1, "v"),
    ("load_wo", 1),
    ("widen", 0, 2, "s"),
    ("load_wo", 0),
    ("quant_s", 0, 0),
    ("turn_h", 0, 0),
    ("empty_bias",),
    ("empty_h", 0, 0, "s"),
    ("turn_h", 0, 1),
    ("load_wos", 1, "g"),
    ("turn_s", 0, 1),
    ("turn_s", 1, 0),
    ("empty_h", 0, 1, "s"),
    ("permute_scales",),
    ("generate", 0, 1),
    ("quant_h", 0, 0),
    ("generate", 0, 0),
    ("empty_s", 0, 1, "s"),
    ("quant_h", 0, 1),
    ("project", 0, 1),
    ("empty_s", 1, 0, "s"),
    ("widen", 1, 2, "s"),
    ("project", 0, 3),
    ("project", 0, 2),
    ("quant_s", 0, 1),
    ("project", 0, 0),
    ("widen", 1, 0, "s"),
    ("empty_gen", 0, 1, "v"),
    ("turn_h", 1, 0),
    ("turn_h", 1, 1),
    ("empty_gen", 0, 0, "v"),
    ("generate", 1, 1),
    ("empty_gain",),
    ("squash", 0, 1),
    ("squash", 0, 3),
    ("squash", 0, 2),
    ("quant_s", 1, 0),
    ("gain", 0, 3, "g"),
    ("generate", 2, 0),
    ("squash", 0, 0),
    ("empty_h", 1, 0, "s"),
    ("empty_h", 1, 1, "s"),
    ("min_gen", 0),
    ("gain", 0, 1, "v"),
    ("gain", 0, 2, "v"),
    ("gain", 0, 0, "v"),
    ("quant_h", 1, 0),
    ("quant_k", 0, 1),
    ("empty_gen", 1, 1, "s"),
    ("quant_k", 0, 0),
    ("generate", 1, 0),
    ("generate", 2, 1),
    ("quant_h", 1, 1),
    ("copy_scores", 0),
    ("exp_gen", 0),
    ("empty_gen", 1, 0, "v"),
    ("project", 1, 3),
    ("empty_gen", 2, 0, "v"),
    ("squash", 1, 3),
    ("empty_gen", 2, 1, "v"),
    ("project", 1, 0),
    ("add_bias", 1, 1),
    ("turn_s", 1, 1),
    ("empty_copy", 0),
    ("project", 1, 2),
    ("min_gen", 1),
    ("gain", 1, 3, "g"),
    ("squash", 1, 0),
    ("gain", 1, 0, "v"),
    ("empty_s", 1, 1, "s"),
    ("exp_copy", 0),
    ("join", 0),
    ("project", 1, 1),
    ("quant_s", 1, 1),
    ("squash", 1, 2),
    ("copy_scores", 1),
    ("empty_copy", 1),
    ("min_gen", 2),
    ("generate", 3, 0),
    ("squash", 1, 1),
    ("exp_gen", 1),
    ("log_a", 0),
    ("exp_copy", 1),
    ("gain", 1, 1, "v"),
    ("gain", 1, 2, "g"),
    ("log_b", 0),
    ("join", 1),
    ("quant_k", 1, 1),
    ("log_c", 0),
    ("exp_gen", 2),
    ("log_a", 1),
    ("quant_k", 1, 0),
    ("log_b", 1),
    ("finish", 0, 2, "s"),
    ("generate", 3, 1),
    ("empty_gen", 3, 0, "v"),
    ("log_c", 1),
    ("finish", 0, 0, "s"),
    ("finish", 1, 0, "s"),
    ("finish", 1, 1, "s"),
    ("store", 0, 2),
    ("empty_gen", 3, 1, "v"),
    ("store", 0, 0),
    ("store", 1, 0),
    ("store", 1, 1),
    ("copy_scores", 2),
    ("empty_copy", 2),
    ("exp_copy", 2),
    ("min_gen", 3),
    ("join", 2),
    ("copy_scores", 3),
    ("log_a", 2),
    ("finish", 1, 2, "g"),
    ("store", 1, 2),
    ("empty_copy", 3),
    ("log_b", 2),
    ("finish", 0, 1, "g"),
    ("log_c", 2),
    ("exp_gen", 3),
    ("finish", 2, 1, "v"),
    ("exp_copy", 3),
    ("store", 0, 1),
    ("join", 3),
    ("finish", 2, 2, "s"),
    ("log_a", 3),
    ("log_b", 3),
    ("log_c", 3),
    ("finish", 3, 0, "v"),
    ("store", 2, 1),
    ("finish", 2, 0, "s"),
    ("finish", 3, 1, "s"),
    ("store", 2, 2),
    ("store", 2, 0),
    ("store", 3, 0),
    ("store", 3, 1),
    ("finish", 3, 2, "s"),
    ("store", 3, 2),
)


def tile_copynetjointgeneratecopyloglift_d2p_kernel(
    tc, h_bytes, h_scale, wc_words, wc_scales, g, s, wo_words, wo_scales, bo, out
):
    nc = tc.nc
    with ExitStack() as ctx:
        keep = ctx.enter_context(tc.tile_pool(name="keep", bufs=1))
        psum = ctx.enter_context(tc.psum_pool(name="psum", bufs=1))
        ctx.enter_context(tc.manual_schedule())

        def sb(name, shape, dtype):
            return keep.tile(shape, dtype, name=name, align_bytes=64)

        free = list(range(8))
        held = {}

        def bank(key, shape, dtype):
            held[key] = free[0]
            free.remove(held[key])
            banks[key] = psum.tile(shape, dtype, name="bank%d" % held[key])

        def release(key):
            free.append(held[key])

        ident = sb("ident", [P, P], F32)
        minus_ones = sb("minus_ones", [P, P], BF16)
        hs = sb("hs", [P, 32], F32)
        hraw = [sb("hraw%d" % b, [P, 4, D], U8) for b in range(B)]
        hwide = [sb("hwide%d" % i, [P, D], BF16) for i in range(8)]
        hgrp = [sb("hgrp%d" % b, [P, T * PACK], BF16) for b in range(B)]
        hq = [sb("hq%d" % b, [P, T], U32) for b in range(B)]
        hqs = [sb("hqs%d" % b, [P, T], U8) for b in range(B)]
        sraw = [sb("sraw%d" % b, [P, 2, D], BF16) for b in range(B)]
        sgrp = [sb("sgrp%d" % b, [P, S * PACK], BF16) for b in range(B)]
        sq = [sb("sq%d" % b, [P, S], U32) for b in range(B)]
        sqs = [sb("sqs%d" % b, [P, S], U8) for b in range(B)]
        wc_raw = sb("wc_raw", [P, 2 * D], U8)
        wcs_raw = sb("wcs_raw", [P, D], U8)
        wc = sb("wc", [P, 2 * D], U8)
        wcs = sb("wcs", [P, D], U8)
        wo = sb("wo", [P, 2 * V], U8)
        wos = sb("wos", [P, V], U8)
        bo_row = sb("bo_row", [P, V], BF16)
        nbias = sb("nbias", [P, V], BF16)
        g4 = sb("g4", [P, PACK], F32)
        g_row = sb("g_row", [P, D], BF16)
        ones = sb("ones", [P, P], BF16)
        series = sb("series", [P, 4, 32], F32)
        th = [sb("th%d" % i, [P, BANK], F32) for i in range(8)]
        kgrp = [sb("kgrp%d" % b, [P, T * PACK], BF16) for b in range(B)]
        kq = [sb("kq%d" % b, [P, T], U32) for b in range(B)]
        kqs = [sb("kqs%d" % b, [P, T], U8) for b in range(B)]
        nz = [sb("nz%d" % i, [P, Z], F32) for i in range(4)]
        res = [sb("res%d" % i, [P, Z], F32) for i in range(4)]
        ngen = [sb("ngen%d" % i, [P, 1], F32) for i in range(4)]
        sgen = [sb("sgen%d" % i, [P, 1], F32) for i in range(4)]
        scopy = [sb("scopy%d" % i, [P, 1], F32) for i in range(4)]
        rescale = [sb("rescale%d" % i, [P, 1], F32) for i in range(4)]
        total = [sb("total%d" % i, [P, 1], F32) for i in range(4)]
        ebits = [sb("ebits%d" % i, [P, 1], I32) for i in range(4)]
        addend = sb("addend", [P, 4, NCOL], F32)
        factor = sb("factor", [P, 4, NCOL], F32)
        horner = [sb("horner%d" % i, [P, NCOL], F32) for i in range(4)]
        banks = {}

        def zero(which):
            nc.vector.memset(dict(wcs=wcs_raw, wos=wos, bo=bo_row, g=g_row, ident=ident)[which][:].bitcast(I32), 0)

        def identity():
            make_identity(nc, ident[:], nomemset=True)

        def constants():
            nc.vector.memset(factor[:], 1.0)
            nc.vector.memset(minus_ones[:], -1.0)
            nc.vector.memset(ones[:], 1.0)

        def constant_term():
            nc.scalar.activation(out=addend[:, :, TERMS], in_=factor[:, :, NCOL - 1], func=ACT.Copy, scale=math.log(Z / CENTRE))

        def coefficients():
            nc.vector.memset(series[:, 0, 0:TERMS], -1.0)
            nc.vector.memset(series[:, 1, 0:TERMS], -CENTRE)
            nc.vector.tensor_tensor_scan(
                out=series[:, 2, 0:TERMS], data0=factor[:, 0, 0:TERMS], data1=series[:, 0, 0:TERMS], initial=TERMS + 1.0, op0=ALU.mult, op1=ALU.add
            )
            nc.vector.tensor_tensor_scan(
                out=series[:, 3, 0:TERMS], data0=series[:, 1, 0:TERMS], data1=factor[:, 0, 0:TERMS], initial=(-1.0 / CENTRE) ** (TERMS + 1), op0=ALU.mult, op1=ALU.mult
            )
            nc.vector.reciprocal(out=series[:, 0, 0:TERMS], in_=series[:, 2, 0:TERMS])
            nc.vector.tensor_tensor(
                out=addend[:, :, 0:TERMS], in0=series[:, 0:1, 0:TERMS].to_broadcast([P, 4, TERMS]),
                in1=series[:, 3:4, 0:TERMS].to_broadcast([P, 4, TERMS]), op=ALU.mult,
            )

        queues = dict(y=nc.sync, s=nc.scalar, g=nc.gpsimd)

        def load_hs(eng):
            queues[eng].dma_start(out=hs[:], in_=h_scale.rearrange("b i j -> (b i j)").partition_broadcast(P))

        def load_h(b, first, count):
            i = slice(first, first + count)
            nc.sync.dma_start(out=hraw[b][:, i, :], in_=h_bytes[b].rearrange("(i p) d -> p i d", p=P)[:, i, :])

        def load_s(b, first, count):
            q = slice(first, first + count)
            nc.sync.dma_start(out=sraw[b][:, q, :], in_=s[b].rearrange("(q p) d -> p q d", p=P)[:, q, :])

        def load_wc():
            nc.sync.dma_start(out=wc_raw[:].bitcast(I32), in_=wc_words[0].bitcast(I32))

        def load_wo(half):
            c = slice(2 * BANK * half, 2 * BANK * (half + 1))
            nc.sync.dma_start(out=wo[:, c].bitcast(I32), in_=wo_words[0][:, c].bitcast(I32))

        def load_wcs(q, eng):
            queues[eng].dma_start(out=wcs_raw[32 * q : 32 * q + 4, :].bitcast(I32), in_=wc_scales[0, 4 * q : 4 * q + 4, :].bitcast(I32))

        def load_wos(q, eng):
            queues[eng].dma_start(out=wos[32 * q : 32 * q + 4, :].bitcast(I32), in_=wo_scales[0, 4 * q : 4 * q + 4, :].bitcast(I32))

        def load_bo(eng):
            queues[eng].dma_start(out=bo_row[0:1, :], in_=bo.rearrange("(o v) -> o v", o=1))

        def load_g(eng):
            queues[eng].dma_start(out=g_row[0:1, :], in_=g.rearrange("(o d) -> o d", o=1))

        def widen(b, i, eng):
            for j in range(4):
                col = 16 * b + 4 * i + j
                src = hraw[b][:, i, P * j : P * (j + 1)].bitcast(FP8)
                dst = hwide[4 * b + i][:, P * j : P * (j + 1)]
                if eng == "s":
                    nc.scalar.activation(out=dst, in_=src, func=ACT.Copy, scale=hs[:, col : col + 1])
                else:
                    nc.vector.tensor_scalar(out=dst, in0=src, scalar1=hs[:, col : col + 1], scalar2=None, op0=ALU.mult)

        def turn(key, tiles):
            bank(key, [P, len(tiles), 2, P], F32)
            for slot, rows in enumerate(tiles):
                words = rows.bitcast(F32)
                for u in range(2):
                    nc.tensor.transpose(banks[key][:, slot, u, :], words[:, u : D // 2 : 2], ident[:])

        def empty_turned(key, dst, eng):
            words = dst.bitcast(F32).rearrange("p (i r u) -> p i r u", r=P, u=2)
            turned = banks[key][:].rearrange("p i u r -> p i r u")
            if eng == "s":
                nc.scalar.copy(out=words, in_=turned)
            else:
                nc.vector.tensor_copy(out=words, in_=turned)
            release(key)

        def turn_h(b, half):
            turn(("h", b, half), [hwide[4 * b + 2 * half + slot][:] for slot in range(2)])

        def empty_h(b, half, eng):
            empty_turned(("h", b, half), hgrp[b][:, 1024 * half : 1024 * (half + 1)], eng)

        def turn_s(b, q):
            turn(("s", b, q), [sraw[b][:, q, :]])

        def empty_s(b, q, eng):
            empty_turned(("s", b, q), sgrp[b][:, BANK * q : BANK * (q + 1)], eng)

        def quant(codes, scales, src):
            nc.vector.quantize_mx(out=codes.bitcast(FP8X4), scales=scales, in_=src)

        def quant_h(b, half):
            c = slice(256 * half, 256 * (half + 1))
            quant(hq[b][:, c], hqs[b][:, c], hgrp[b][:, 1024 * half : 1024 * (half + 1)])

        def quant_k(b, half):
            c = slice(256 * half, 256 * (half + 1))
            quant(kq[b][:, c], kqs[b][:, c], kgrp[b][:, 1024 * half : 1024 * (half + 1)])

        def project(b, c):
            bank(("p", b, c), [P, PACK, P], F32)
            cols = slice(P * c, P * (c + 1))
            for t in range(PACK):
                nc.tensor.matmul_mx(
                    out=banks["p", b, c][:, t, :],
                    lhsT=wc[:, 2 * P * t : 2 * P * (t + 1)].bitcast(FP4X4),
                    lhsT_scale=wcs[:, P * t : P * (t + 1)],
                    rhs=hq[b][:, cols].bitcast(FP8X4),
                    rhs_scale=hqs[b][:, cols],
                    start=True,
                    stop=True,
                )

        def squash(b, c):
            nc.scalar.activation(
                out=th[4 * b + c][:].rearrange("p (n t) -> p n t", t=PACK),
                in_=banks["p", b, c][:].rearrange("p t n -> p n t"),
                func=ACT.Tanh,
            )
            release(("p", b, c))

        def gain(b, c, eng):
            dst = kgrp[b][:, BANK * c : BANK * (c + 1)]
            if eng == "v":
                nc.vector.tensor_tensor(
                    out=dst, in0=th[4 * b + c][:], in1=banks["gain"][:].rearrange("p n t -> p (n t)"), op=ALU.mult
                )
            else:
                nc.gpsimd.tensor_tensor(
                    out=dst.rearrange("p (n t) -> p n t", t=PACK),
                    in0=th[4 * b + c][:].rearrange("p (n t) -> p n t", t=PACK),
                    in1=g4[:].unsqueeze(1).to_broadcast([P, P, PACK]),
                    op=ALU.mult,
                )

        def empty_gain():
            nc.vector.tensor_copy(out=g4[:], in_=banks["gain"][:, 0, :])

        def generate(n, half):
            b, q = divmod(n, 2)
            rows = slice(P * q, P * (q + 1))
            bank(("g", n, half), [P, BANK], F32)
            nc.tensor.matmul_mx(
                out=banks["g", n, half][:],
                lhsT=sq[b][:, rows].bitcast(FP8X4),
                lhsT_scale=sqs[b][:, rows],
                rhs=wo[:, 2 * BANK * half : 2 * BANK * (half + 1)].bitcast(FP4X4),
                rhs_scale=wos[:, BANK * half : BANK * (half + 1)],
                start=True,
                stop=True,
            )

        def empty_gen(n, half, eng):
            c = slice(BANK * half, BANK * (half + 1))
            if eng == "v":
                nc.vector.tensor_tensor(out=nz[n][:, c], in0=nbias[:, c], in1=banks["g", n, half][:], op=ALU.subtract)
            else:
                nc.scalar.activation(out=nz[n][:, c], in_=banks["g", n, half][:], func=ACT.Copy, scale=-1.0)
            release(("g", n, half))

        def add_bias(n, half):
            c = slice(BANK * half, BANK * (half + 1))
            nc.gpsimd.tensor_tensor(out=nz[n][:, c], in0=nz[n][:, c], in1=nbias[:, c], op=ALU.add)

        def min_gen(n):
            nc.vector.tensor_reduce(out=ngen[n][:], in_=nz[n][:, 0:V], axis=AX.X, op=ALU.min)

        def copy_scores(n):
            b, q = divmod(n, 2)
            rows = slice(P * q, P * (q + 1))
            bank(("c", n), [P, BANK], F32)
            nc.tensor.matmul_mx(
                out=banks["c", n][:],
                lhsT=sq[b][:, rows].bitcast(FP8X4),
                lhsT_scale=sqs[b][:, rows],
                rhs=kq[b][:].bitcast(FP8X4),
                rhs_scale=kqs[b][:],
                start=True,
                stop=True,
            )

        def empty_copy(n):
            nc.vector.tensor_scalar(
                out=nz[n][:, V:Z],
                in0=banks["c", n][:],
                scalar1=-1.0 / math.sqrt(D),
                scalar2=ngen[n][:],
                op0=ALU.mult,
                op1=ALU.min,
                accum_out=addend[:, n, NCOL - 1 : NCOL],
            )
            release(("c", n))

        def exp_gen(n):
            nc.scalar.activation(
                out=res[n][:, 0:V], in_=nz[n][:, 0:V], func=ACT.Exp, scale=-1.0, bias=ngen[n][:], accum_out=sgen[n][:]
            )

        def exp_copy(n):
            shift = addend[:, n, NCOL - 1 : NCOL]
            nc.scalar.activation(out=rescale[n][:], in_=ngen[n][:], func=ACT.Exp, scale=-1.0, bias=shift)
            nc.scalar.activation(out=res[n][:, V:Z], in_=nz[n][:, V:Z], func=ACT.Exp, scale=-1.0, bias=shift, accum_out=scopy[n][:])

        def join(n):
            nc.vector.tensor_scalar(
                out=total[n][:], in0=sgen[n][:], scalar1=rescale[n][:], scalar2=scopy[n][:], op0=ALU.mult, op1=ALU.add
            )

        def log_a(n):
            nc.vector.tensor_scalar(
                out=ebits[n][:], in0=total[n][:].bitcast(I32), scalar1=EXP_MASK, scalar2=EXP_MASK,
                op0=ALU.bitwise_xor, op1=ALU.bitwise_and,
            )

        def log_b(n):
            nc.vector.tensor_scalar(
                out=factor[:, n, 0 : TERMS + 1], in0=ebits[n][:].bitcast(F32).to_broadcast([P, TERMS + 1]),
                scalar1=total[n][:], scalar2=-CENTRE, op0=ALU.mult, op1=ALU.add,
            )
            nc.vector.tensor_scalar(
                out=addend[:, n, TERMS + 1 : TERMS + 2], in0=ebits[n][:],
                scalar1=-127.0 * 2.0**23, scalar2=math.log(2.0) / 2.0**23, op0=ALU.add, op1=ALU.mult,
            )

        def log_c(n):
            nc.vector.tensor_tensor_scan(
                out=horner[n][:], data0=factor[:, n, :], data1=addend[:, n, :], initial=0.0, op0=ALU.mult, op1=ALU.add
            )

        def finish(n, part, eng):
            c0, c1 = BANK * part, BANK * (part + 1)
            shift = horner[n][:, NCOL - 1 : NCOL]
            if eng == "s":
                nc.scalar.activation(out=res[n][:, c0:c1], in_=nz[n][:, c0:c1], func=ACT.Identity, scale=-1.0, bias=shift)
            else:
                e = nc.gpsimd if eng == "g" else nc.vector
                e.tensor_scalar(out=res[n][:, c0:c1], in0=nz[n][:, c0:c1], scalar1=-1.0, scalar2=shift, op0=ALU.mult, op1=ALU.add)

        def store(n, part):
            b, q = divmod(n, 2)
            c0, c1 = BANK * part, BANK * (part + 1)
            nc.sync.dma_start(out=out[b, P * q : P * (q + 1), c0:c1], in_=res[n][:, c0:c1])

        def permute_words():
            nc.vector.tensor_copy(
                out=wc[:].rearrange("p (t m e) -> p t m e", t=PACK, e=2), in_=wc_raw[:].rearrange("p (m t e) -> p t m e", t=PACK, e=2)
            )

        def permute_scales():
            nc.vector.tensor_copy(
                out=wcs[:].rearrange("p (t m) -> p t m", t=PACK), in_=wcs_raw[:].rearrange("p (m t) -> p t m", t=PACK)
            )

        def spread_bias():
            bank("bias", [P, V], BF16)
            for half in range(2):
                c = slice(BANK * half, BANK * (half + 1))
                nc.tensor.matmul(out=banks["bias"][:, c], lhsT=minus_ones[:], rhs=bo_row[:, c], start=True, stop=True)

        def empty_bias():
            nc.scalar.copy(out=nbias[:], in_=banks["bias"][:])
            release("bias")

        def repeat_gain():
            bank("gain", [P, P, PACK], F32)
            for t in range(PACK):
                nc.tensor.matmul(out=banks["gain"][:, :, t], lhsT=g_row[:, t:D:PACK], rhs=ones[:], start=True, stop=True)

        def quant_s(b, q):
            c = slice(P * q, P * (q + 1))
            quant(sq[b][:, c], sqs[b][:, c], sgrp[b][:, BANK * q : BANK * (q + 1)])

        steps = dict(
            widen=widen, turn_h=turn_h, turn_s=turn_s, empty_h=empty_h, empty_s=empty_s, quant_h=quant_h, quant_s=quant_s,
            quant_k=quant_k, project=project, squash=squash, gain=gain, empty_gain=empty_gain, generate=generate, add_bias=add_bias, empty_gen=empty_gen, min_gen=min_gen,
            copy_scores=copy_scores, empty_copy=empty_copy, exp_gen=exp_gen, exp_copy=exp_copy, join=join, store=store, load_hs=load_hs, load_h=load_h, load_s=load_s,
            load_wc=load_wc, load_wo=load_wo, load_wcs=load_wcs, load_wos=load_wos, load_bo=load_bo, load_g=load_g, log_a=log_a, log_b=log_b, log_c=log_c, finish=finish,
            permute_words=permute_words, permute_scales=permute_scales, spread_bias=spread_bias, empty_bias=empty_bias,
            repeat_gain=repeat_gain, zero=zero, identity=identity, constants=constants, constant_term=constant_term,
            coefficients=coefficients,
        )
        for name, *args in ORDER:
            steps[name](*args)
